import numpy as np, ml_dtypes
CORES = [78,86,94,102,110,118]
N = 6
S, B = 4, 128
def setup_inputs(rng):
    return {"x": rng.standard_normal((N, 128, S * B), dtype=np.float32).astype(ml_dtypes.bfloat16), "gate": (0.9375 + 0.03125 * rng.standard_normal((N, 128, S * B), dtype=np.float32)).astype(ml_dtypes.bfloat16)}
def setup_inputs_big(rng):
    d = setup_inputs(rng)
    for k in ("x",): d[k] = (d[k].astype(np.float32) * 1048576.0).astype(d[k].dtype)
    return d
def setup_inputs_small(rng):
    d = setup_inputs(rng)
    for k in ("x",): d[k] = (d[k].astype(np.float32) * (1 / 1048576.0)).astype(d[k].dtype)
    return d
def setup_inputs_apart(rng):
    d = setup_inputs(rng)
    f = (10.0 ** rng.permutation(np.linspace(-1.5, 1.5, N))).astype(np.float32).reshape(N, 1, 1)
    for k in ("x",): d[k] = (d[k].astype(np.float32) * f).astype(d[k].dtype)
    return d
def reference(x, gate):
    X, GATE = x.astype(np.float64), gate.astype(np.float64)
    y = np.zeros((N, 128, S * B)); h = np.zeros((128, B))
    for r in range(N):
        for s in range(S):
            h = GATE[r][:, B * s:B * s + B] * h + X[r][:, B * s:B * s + B]
            y[r][:, B * s:B * s + B] = h
    return {"y": y.astype(ml_dtypes.bfloat16)}

@@ -1,0 +1,207 @@
+from concourse.bass import DstId, RemoteDMATransfer
+from concourse.mybir import AluOpType
+
+B = 128
+S = 4
+
+VAL_DESTS = {0: [1, 2, 3, 4, 5]}
+PAIR_DESTS = {1: [2, 3, 4, 5], 2: [3, 4, 5], 3: [4, 5], 4: [5]}
+
+SCRATCH = {
+    "xs": ("sbuf", [128, S * B], "bfloat16"),
+    "gs": ("sbuf", [128, S * B], "bfloat16"),
+    "ab": ("sbuf", [128, 2 * B], "bfloat16"),
+    "ys": ("sbuf", [128, S * B], "bfloat16"),
+    "ts": ("sbuf", [128, S * B], "bfloat16"),
+    "tq": ("sbuf", [128, 4 * B], "bfloat16"),
+    "cs": ("sbuf", [128, B], "bfloat16"),
+    "pland": ("sbuf", [128, 4 * 2 * B], "bfloat16"),
+    "vland": ("sbuf", [128, B], "bfloat16"),
+    "Pp": ("psum", [128, S * B], "float32"),
+    "Lp": ("psum", [128, S * B], "float32"),
+    "Mp": ("psum", [128, 4 * B], "float32"),
+    "Qp": ("psum", [128, 4 * B], "float32"),
+    "Dp": ("psum", [128, 4 * B], "float32"),
+}
+SEMAPHORES = ["ldx", "ldg", "v", "abr", "y3r", "yh0", "yh1", "st0", "st1", "sent", "av", "ap1", "ap2", "ap3", "ap4"]
+
+
+def rank_program(g, core, T, topo):
+    r = T.rank_of(core)
+    if r is None:
+        return
+    V = g.vector
+    sem = T.sem
+    cores = T.cores
+    mult, add = AluOpType.mult, AluOpType.add
+
+    val_dests = VAL_DESTS.get(r, [])
+    pair_dests = PAIR_DESTS.get(r, [])
+    m = None
+    for k in VAL_DESTS:
+        if r in VAL_DESTS[k]:
+            m = k + 1
+
+    def engines(src_rank, dests):
+        mk = None
+        for j in dests:
+            if not topo.may_write(cores[src_rank], cores[j]):
+                raise ValueError("rank %d may not write to rank %d" % (src_rank, j))
+            one = topo.mask(cores[src_rank], cores[j])
+            mk = one if mk is None else (mk & one)
+        return mk, bin(mk).count("1")
+
+    g0 = 0 if r > 0 else B
+    g.sync.dma_start(T.gs[:, g0:S * B], T.gate[:, g0:S * B]).then_inc(sem.ldg, 16)
+    g.scalar.dma_start(T.xs[:], T.x[:]).then_inc(sem.ldx, 16)
+
+    counts = {}
+    waited = {}
+    dirty = []
+
+    def ap(rg):
+        return T[rg[0]][:, rg[1]:rg[2]]
+
+    def blk(name, i, n=1):
+        return (name, i * B, (i + n) * B)
+
+    def fence():
+        for s in counts:
+            if waited.get(s, 0) < counts[s]:
+                V.wait_ge(sem[s], counts[s])
+                waited[s] = counts[s]
+        del dirty[:]
+
+    def need(regs):
+        for a in regs:
+            for d in dirty:
+                if a[0] == d[0] and a[1] < d[2] and d[1] < a[2]:
+                    fence()
+                    return
+
+    def done(ins, out, s):
+        ins.then_inc(sem[s], 1)
+        counts[s] = counts.get(s, 0) + 1
+        dirty.append(out)
+
+    def tt(out, a, b, op, s="v"):
+        need([a, b, out])
+        done(V.tensor_tensor(ap(out), ap(a), ap(b), op), out, s)
+
+    def cp(out, a, s="v"):
+        need([a, out])
+        done(V.tensor_copy(ap(out), ap(a)), out, s)
+
+    def G(i):
+        return blk("gs", i)
+
+    def X(i):
+        return blk("xs", i)
+
+    V.wait_ge(sem.ldg, 16)
+    if r > 0:
+        tt(blk("Pp", 1), G(0), G(1), mult)
+        tt(blk("Pp", 2), blk("Pp", 1), G(2), mult)
+        if pair_dests:
+            tt(blk("ab", 0), blk("Pp", 2), G(3), mult, "abr")
+        else:
+            tt(blk("Pp", 3), blk("Pp", 2), G(3), mult)
+    V.wait_ge(sem.ldx, 16)
+    tt(blk("Mp", 0), G(1), X(0), mult)
+    tt(blk("Lp", 1), blk("Mp", 0), X(1), add)
+    tt(blk("Mp", 1), blk("Lp", 1), G(2), mult)
+    tt(blk("Lp", 2), blk("Mp", 1), X(2), add)
+    tt(blk("Mp", 2), blk("Lp", 2), G(3), mult)
+    if r == 0:
+        tt(blk("ys", 3), blk("Mp", 2), X(3), add, "y3r")
+    elif pair_dests:
+        tt(blk("ab", 1), blk("Mp", 2), X(3), add, "abr")
+    else:
+        tt(blk("Lp", 3), blk("Mp", 2), X(3), add)
+
+    half = {0: [], 1: []}
+    if r == 0:
+        cp(blk("ys", 2), blk("Lp", 2), "yh1")
+        cp(blk("ys", 0), X(0), "yh0")
+        cp(blk("ys", 1), blk("Lp", 1), "yh0")
+        half[0] = ["yh0"]
+        half[1] = ["yh1", "y3r"]
+    else:
+        if pair_dests:
+            tt(blk("Pp", 3), blk("Pp", 2), G(3), mult)
+            tt(blk("Lp", 3), blk("Mp", 2), X(3), add)
+        cp(blk("Pp", 0), G(0))
+        cp(blk("Lp", 0), X(0))
+
+        def arrived(name, src_rank, dests):
+            V.wait_ge(sem[name], engines(src_rank, dests)[1])
+
+        def landed(k):
+            arrived("ap%d" % k, k, PAIR_DESTS[k])
+            return blk("pland", 2 * (k - 1)), blk("pland", 2 * (k - 1) + 1)
+
+        val = blk("vland", 0)
+        if m == r:
+            arrived("av", m - 1, VAL_DESTS[m - 1])
+            c = val
+        else:
+            Q, d = landed(r - 1)
+            d_sbuf = True
+            i = 0
+            for k in range(r - 2, m - 1, -1):
+                Ak, bk = landed(k)
+                t = blk("Mp", 3) if d_sbuf else blk("tq", i)
+                tt(t, Q, bk, mult)
+                tt(blk("Qp", i), Q, Ak, mult)
+                tt(blk("Dp", i), t, d, add)
+                Q, d, d_sbuf = blk("Qp", i), blk("Dp", i), False
+                i += 1
+            arrived("av", m - 1, VAL_DESTS[m - 1])
+            t = blk("Mp", 3) if d_sbuf else blk("tq", i)
+            tt(t, Q, val, mult)
+            c = blk("cs", 0)
+            tt(c, t, d, add)
+
+        if val_dests:
+            tt(blk("ts", 3), blk("Pp", 3), c, mult)
+            tt(blk("ys", 3), blk("ts", 3), blk("Lp", 3), add, "y3r")
+            tt(blk("ts", 2), blk("Pp", 2), c, mult)
+            tt(blk("ys", 2), blk("ts", 2), blk("Lp", 2), add, "yh1")
+            half[1] = ["yh1", "y3r"]
+            tt(blk("ts", 0), blk("Pp", 0), c, mult)
+            tt(blk("ts", 1), blk("Pp", 1), c, mult)
+            tt(blk("ys", 0, 2), blk("ts", 0, 2), blk("Lp", 0, 2), add, "yh0")
+            half[0] = ["yh0"]
+        else:
+            for h in (0, 1):
+                tt(blk("ts", 2 * h), blk("Pp", 2 * h), c, mult)
+                tt(blk("ts", 2 * h + 1), blk("Pp", 2 * h + 1), c, mult)
+                tt(blk("ys", 2 * h, 2), blk("ts", 2 * h, 2), blk("Lp", 2 * h, 2), add, "yh%d" % h)
+                half[h] = ["yh%d" % h]
+    fence()
+
+    def send(src, dst, dests, rsem):
+        mk, n = engines(r, dests)
+        ids = []
+        for j in dests:
+            a = topo.addr(cores[j])
+            ids.append(DstId(rid=a[0], pnc=a[1]))
+        g.remote_dma_fused([RemoteDMATransfer(dst_ids=ids, dma_engine_mask=mk, remote_sem=rsem, srcs=[ap(src)],
+                                              dsts=[ap(dst) for j in dests], alu_op=0)], local_sem=sem.sent)
+        return n
+
+    left = 0
+    if pair_dests:
+        g.wait_ge(sem.abr, counts["abr"])
+        left += send(blk("ab", 0, 2), blk("pland", 2 * (r - 1), 2), pair_dests, sem["ap%d" % r])
+    if val_dests:
+        g.wait_ge(sem.y3r, counts["y3r"])
+        left += send(blk("ys", 3), blk("vland", 0), val_dests, sem.av)
+    if left:
+        g.wait_ge(sem.sent, left)
+
+    for h, q, st in ((0, g.sync, sem.st0), (1, g.scalar, sem.st1)):
+        for s in half[h]:
+            q.wait_ge(sem[s], counts[s])
+        q.dma_start(T.y[:, 2 * h * B:(2 * h + 2) * B], T.ys[:, 2 * h * B:(2 * h + 2) * B]).then_inc(st, 16)
+        q.wait_ge(st, 16)

@@ -23,7 +23,8 @@ SCRATCH = {
     "Qp": ("psum", [128, 4 * B], "float32"),
     "Dp": ("psum", [128, 4 * B], "float32"),
 }
-SEMAPHORES = ["ldx", "ldg", "v", "abr", "y3r", "yh0", "yh1", "st0", "st1", "sent", "av", "ap1", "ap2", "ap3", "ap4"]
+SEMAPHORES = ["ldx", "ldg", "va", "vb", "abr", "y3r", "yh0", "yh1", "st0", "st1", "sent", "av",
+              "ap1", "ap2", "ap3", "ap4"]
 
 
 def rank_program(g, core, T, topo):
@@ -34,13 +35,8 @@ def rank_program(g, core, T, topo):
     sem = T.sem
     cores = T.cores
     mult, add = AluOpType.mult, AluOpType.add
-
     val_dests = VAL_DESTS.get(r, [])
     pair_dests = PAIR_DESTS.get(r, [])
-    m = None
-    for k in VAL_DESTS:
-        if r in VAL_DESTS[k]:
-            m = k + 1
 
     def engines(src_rank, dests):
         mk = None
@@ -65,30 +61,28 @@ def rank_program(g, core, T, topo):
     def blk(name, i, n=1):
         return (name, i * B, (i + n) * B)
 
-    def fence():
-        for s in counts:
-            if waited.get(s, 0) < counts[s]:
-                V.wait_ge(sem[s], counts[s])
-                waited[s] = counts[s]
-        del dirty[:]
+    def wait_whole(s):
+        if waited.get(s, 0) < counts[s]:
+            V.wait_ge(sem[s], counts[s])
+            waited[s] = counts[s]
+        dirty[:] = [e for e in dirty if e[1] != s]
 
     def need(regs):
         for a in regs:
-            for d in dirty:
+            for d, s in list(dirty):
                 if a[0] == d[0] and a[1] < d[2] and d[1] < a[2]:
-                    fence()
-                    return
+                    wait_whole(s)
 
     def done(ins, out, s):
         ins.then_inc(sem[s], 1)
         counts[s] = counts.get(s, 0) + 1
-        dirty.append(out)
+        dirty.append((out, s))
 
-    def tt(out, a, b, op, s="v"):
+    def tt(s, out, a, b, op):
         need([a, b, out])
         done(V.tensor_tensor(ap(out), ap(a), ap(b), op), out, s)
 
-    def cp(out, a, s="v"):
+    def cp(s, out, a):
         need([a, out])
         done(V.tensor_copy(ap(out), ap(a)), out, s)
 
@@ -99,86 +93,75 @@ def rank_program(g, core, T, topo):
         return blk("xs", i)
 
     V.wait_ge(sem.ldg, 16)
-    if r > 0:
-        tt(blk("Pp", 1), G(0), G(1), mult)
-        tt(blk("Pp", 2), blk("Pp", 1), G(2), mult)
-        if pair_dests:
-            tt(blk("ab", 0), blk("Pp", 2), G(3), mult, "abr")
-        else:
-            tt(blk("Pp", 3), blk("Pp", 2), G(3), mult)
     V.wait_ge(sem.ldx, 16)
-    tt(blk("Mp", 0), G(1), X(0), mult)
-    tt(blk("Lp", 1), blk("Mp", 0), X(1), add)
-    tt(blk("Mp", 1), blk("Lp", 1), G(2), mult)
-    tt(blk("Lp", 2), blk("Mp", 1), X(2), add)
-    tt(blk("Mp", 2), blk("Lp", 2), G(3), mult)
+    if r > 0:
+        tt("va", blk("Pp", 1), G(0), G(1), mult)
+    tt("vb", blk("Mp", 0), G(1), X(0), mult)
+    if r > 0:
+        tt("va", blk("Pp", 2), blk("Pp", 1), G(2), mult)
+    tt("vb", blk("Lp", 1), blk("Mp", 0), X(1), add)
+    if pair_dests:
+        tt("abr", blk("ab", 0), blk("Pp", 2), G(3), mult)
+    elif r > 0:
+        tt("va", blk("Pp", 3), blk("Pp", 2), G(3), mult)
+    tt("vb", blk("Mp", 1), blk("Lp", 1), G(2), mult)
+    tt("vb", blk("Lp", 2), blk("Mp", 1), X(2), add)
+    tt("vb", blk("Mp", 2), blk("Lp", 2), G(3), mult)
     if r == 0:
-        tt(blk("ys", 3), blk("Mp", 2), X(3), add, "y3r")
+        tt("y3r", blk("ys", 3), blk("Mp", 2), X(3), add)
     elif pair_dests:
-        tt(blk("ab", 1), blk("Mp", 2), X(3), add, "abr")
+        tt("abr", blk("ab", 1), blk("Mp", 2), X(3), add)
     else:
-        tt(blk("Lp", 3), blk("Mp", 2), X(3), add)
+        tt("vb", blk("Lp", 3), blk("Mp", 2), X(3), add)
 
-    half = {0: [], 1: []}
     if r == 0:
-        cp(blk("ys", 2), blk("Lp", 2), "yh1")
-        cp(blk("ys", 0), X(0), "yh0")
-        cp(blk("ys", 1), blk("Lp", 1), "yh0")
-        half[0] = ["yh0"]
-        half[1] = ["yh1", "y3r"]
+        cp("yh1", blk("ys", 2), blk("Lp", 2))
+        cp("yh0", blk("ys", 0), X(0))
+        cp("yh0", blk("ys", 1), blk("Lp", 1))
+        half = {0: ["yh0"], 1: ["yh1", "y3r"]}
     else:
         if pair_dests:
-            tt(blk("Pp", 3), blk("Pp", 2), G(3), mult)
-            tt(blk("Lp", 3), blk("Mp", 2), X(3), add)
-        cp(blk("Pp", 0), G(0))
-        cp(blk("Lp", 0), X(0))
-
-        def arrived(name, src_rank, dests):
-            V.wait_ge(sem[name], engines(src_rank, dests)[1])
+            tt("va", blk("Pp", 3), blk("Pp", 2), G(3), mult)
+            tt("vb", blk("Lp", 3), blk("Mp", 2), X(3), add)
+        cp("va", blk("Pp", 0), G(0))
+        cp("vb", blk("Lp", 0), X(0))
 
         def landed(k):
-            arrived("ap%d" % k, k, PAIR_DESTS[k])
+            V.wait_ge(sem["ap%d" % k], engines(k, PAIR_DESTS[k])[1])
             return blk("pland", 2 * (k - 1)), blk("pland", 2 * (k - 1) + 1)
 
+        n_val = engines(0, VAL_DESTS[0])[1]
         val = blk("vland", 0)
-        if m == r:
-            arrived("av", m - 1, VAL_DESTS[m - 1])
+        if r == 1:
+            V.wait_ge(sem.av, n_val)
             c = val
         else:
             Q, d = landed(r - 1)
             d_sbuf = True
             i = 0
-            for k in range(r - 2, m - 1, -1):
+            for k in range(r - 2, 0, -1):
                 Ak, bk = landed(k)
                 t = blk("Mp", 3) if d_sbuf else blk("tq", i)
-                tt(t, Q, bk, mult)
-                tt(blk("Qp", i), Q, Ak, mult)
-                tt(blk("Dp", i), t, d, add)
+                tt("vb", t, Q, bk, mult)
+                tt("va", blk("Qp", i), Q, Ak, mult)
+                tt("vb", blk("Dp", i), t, d, add)
                 Q, d, d_sbuf = blk("Qp", i), blk("Dp", i), False
                 i += 1
-            arrived("av", m - 1, VAL_DESTS[m - 1])
+            V.wait_ge(sem.av, n_val)
             t = blk("Mp", 3) if d_sbuf else blk("tq", i)
-            tt(t, Q, val, mult)
+            tt("vb", t, Q, val, mult)
             c = blk("cs", 0)
-            tt(c, t, d, add)
+            tt("vb", c, t, d, add)
 
-        if val_dests:
-            tt(blk("ts", 3), blk("Pp", 3), c, mult)
-            tt(blk("ys", 3), blk("ts", 3), blk("Lp", 3), add, "y3r")
-            tt(blk("ts", 2), blk("Pp", 2), c, mult)
-            tt(blk("ys", 2), blk("ts", 2), blk("Lp", 2), add, "yh1")
-            half[1] = ["yh1", "y3r"]
-            tt(blk("ts", 0), blk("Pp", 0), c, mult)
-            tt(blk("ts", 1), blk("Pp", 1), c, mult)
-            tt(blk("ys", 0, 2), blk("ts", 0, 2), blk("Lp", 0, 2), add, "yh0")
-            half[0] = ["yh0"]
-        else:
-            for h in (0, 1):
-                tt(blk("ts", 2 * h), blk("Pp", 2 * h), c, mult)
-                tt(blk("ts", 2 * h + 1), blk("Pp", 2 * h + 1), c, mult)
-                tt(blk("ys", 2 * h, 2), blk("ts", 2 * h, 2), blk("Lp", 2 * h, 2), add, "yh%d" % h)
-                half[h] = ["yh%d" % h]
-    fence()
+        tt("va", blk("ts", 0), blk("Pp", 0), c, mult)
+        tt("va", blk("ts", 1), blk("Pp", 1), c, mult)
+        tt("vb", blk("ts", 2), blk("Pp", 2), c, mult)
+        tt("vb", blk("ts", 3), blk("Pp", 3), c, mult)
+        tt("yh0", blk("ys", 0, 2), blk("ts", 0, 2), blk("Lp", 0, 2), add)
+        tt("yh1", blk("ys", 2, 2), blk("ts", 2, 2), blk("Lp", 2, 2), add)
+        half = {0: ["yh0"], 1: ["yh1"]}
+    for s in list(counts):
+        wait_whole(s)
 
     def send(src, dst, dests, rsem):
         mk, n = engines(r, dests)
@@ -190,15 +173,12 @@ def rank_program(g, core, T, topo):
                                               dsts=[ap(dst) for j in dests], alu_op=0)], local_sem=sem.sent)
         return n
 
-    left = 0
     if pair_dests:
         g.wait_ge(sem.abr, counts["abr"])
-        left += send(blk("ab", 0, 2), blk("pland", 2 * (r - 1), 2), pair_dests, sem["ap%d" % r])
+        g.wait_ge(sem.sent, send(blk("ab", 0, 2), blk("pland", 2 * (r - 1), 2), pair_dests, sem["ap%d" % r]))
     if val_dests:
         g.wait_ge(sem.y3r, counts["y3r"])
-        left += send(blk("ys", 3), blk("vland", 0), val_dests, sem.av)
-    if left:
-        g.wait_ge(sem.sent, left)
+        g.wait_ge(sem.sent, send(blk("ys", 3), blk("vland", 0), val_dests, sem.av))
 
     for h, q, st in ((0, g.sync, sem.st0), (1, g.scalar, sem.st1)):
         for s in half[h]:

@@ -3,6 +3,7 @@ from concourse.mybir import AluOpType
 
 B = 128
 S = 4
+NV = 40
 
 VAL_DESTS = {0: [1, 2, 3, 4, 5]}
 PAIR_DESTS = {1: [2, 3, 4, 5], 2: [3, 4, 5], 3: [4, 5], 4: [5]}
@@ -10,6 +11,8 @@ PAIR_DESTS = {1: [2, 3, 4, 5], 2: [3, 4, 5], 3: [4, 5], 4: [5]}
 SCRATCH = {
     "xs": ("sbuf", [128, S * B], "bfloat16"),
     "gs": ("sbuf", [128, S * B], "bfloat16"),
+    "gg": ("sbuf", [128, B], "bfloat16"),
+    "bb": ("sbuf", [128, B], "bfloat16"),
     "ab": ("sbuf", [128, 2 * B], "bfloat16"),
     "ys": ("sbuf", [128, S * B], "bfloat16"),
     "ts": ("sbuf", [128, S * B], "bfloat16"),
@@ -20,11 +23,12 @@ SCRATCH = {
     "Pp": ("psum", [128, S * B], "float32"),
     "Lp": ("psum", [128, S * B], "float32"),
     "Mp": ("psum", [128, 4 * B], "float32"),
+    "Rp": ("psum", [128, B], "float32"),
     "Qp": ("psum", [128, 4 * B], "float32"),
     "Dp": ("psum", [128, 4 * B], "float32"),
 }
-SEMAPHORES = ["ldx", "ldg", "va", "vb", "abr", "y3r", "yh0", "yh1", "st0", "st1", "sent", "av",
-              "ap1", "ap2", "ap3", "ap4"]
+SEMAPHORES = ["ldx", "ldg", "abr", "y3r", "yh0", "yh1", "st0", "st1", "sent", "av",
+              "ap1", "ap2", "ap3", "ap4"] + ["s%d" % i for i in range(NV)]
 
 
 def rank_program(g, core, T, topo):
@@ -52,7 +56,6 @@ def rank_program(g, core, T, topo):
     g.scalar.dma_start(T.xs[:], T.x[:]).then_inc(sem.ldx, 16)
 
     counts = {}
-    waited = {}
     dirty = []
 
     def ap(rg):
@@ -61,28 +64,26 @@ def rank_program(g, core, T, topo):
     def blk(name, i, n=1):
         return (name, i * B, (i + n) * B)
 
-    def wait_whole(s):
-        if waited.get(s, 0) < counts[s]:
-            V.wait_ge(sem[s], counts[s])
-            waited[s] = counts[s]
-        dirty[:] = [e for e in dirty if e[1] != s]
-
     def need(regs):
         for a in regs:
-            for d, s in list(dirty):
-                if a[0] == d[0] and a[1] < d[2] and d[1] < a[2]:
-                    wait_whole(s)
+            for e in list(dirty):
+                d = e[0]
+                if a[0] == d[0] and a[1] < d[2] and d[1] < a[2] and e in dirty:
+                    V.wait_ge(sem[e[1]], counts[e[1]])
+                    dirty[:] = [f for f in dirty if f[1] != e[1]]
 
     def done(ins, out, s):
+        if s is None:
+            s = "s%d" % len([q for q in counts if q[0] == "s" and q[1:].isdigit()])
         ins.then_inc(sem[s], 1)
         counts[s] = counts.get(s, 0) + 1
         dirty.append((out, s))
 
-    def tt(s, out, a, b, op):
+    def tt(out, a, b, op, s=None):
         need([a, b, out])
         done(V.tensor_tensor(ap(out), ap(a), ap(b), op), out, s)
 
-    def cp(s, out, a):
+    def cp(out, a, s=None):
         need([a, out])
         done(V.tensor_copy(ap(out), ap(a)), out, s)
 
@@ -92,40 +93,39 @@ def rank_program(g, core, T, topo):
     def X(i):
         return blk("xs", i)
 
+    gg, bb = blk("gg", 0), blk("bb", 0)
+
     V.wait_ge(sem.ldg, 16)
     V.wait_ge(sem.ldx, 16)
+    tt(blk("Mp", 0), G(1), X(0), mult)
+    tt(gg, G(2), G(3), mult)
+    tt(blk("Mp", 1), G(3), X(2), mult)
+    tt(blk("Lp", 1), blk("Mp", 0), X(1), add)
     if r > 0:
-        tt("va", blk("Pp", 1), G(0), G(1), mult)
-    tt("vb", blk("Mp", 0), G(1), X(0), mult)
-    if r > 0:
-        tt("va", blk("Pp", 2), blk("Pp", 1), G(2), mult)
-    tt("vb", blk("Lp", 1), blk("Mp", 0), X(1), add)
+        tt(blk("Pp", 1), G(0), G(1), mult)
+    tt(bb, blk("Mp", 1), X(3), add)
+    tt(blk("Mp", 2), blk("Lp", 1), gg, mult)
     if pair_dests:
-        tt("abr", blk("ab", 0), blk("Pp", 2), G(3), mult)
-    elif r > 0:
-        tt("va", blk("Pp", 3), blk("Pp", 2), G(3), mult)
-    tt("vb", blk("Mp", 1), blk("Lp", 1), G(2), mult)
-    tt("vb", blk("Lp", 2), blk("Mp", 1), X(2), add)
-    tt("vb", blk("Mp", 2), blk("Lp", 2), G(3), mult)
+        tt(blk("ab", 0), blk("Pp", 1), gg, mult, "abr")
+        tt(blk("ab", 1), blk("Mp", 2), bb, add, "abr")
     if r == 0:
-        tt("y3r", blk("ys", 3), blk("Mp", 2), X(3), add)
-    elif pair_dests:
-        tt("abr", blk("ab", 1), blk("Mp", 2), X(3), add)
-    else:
-        tt("vb", blk("Lp", 3), blk("Mp", 2), X(3), add)
+        tt(blk("ys", 3), blk("Mp", 2), bb, add, "y3r")
+
+    tt(blk("Mp", 3), blk("Lp", 1), G(2), mult)
+    if r > 0:
+        tt(blk("Pp", 2), blk("Pp", 1), G(2), mult)
+        tt(blk("Pp", 3), blk("Pp", 1), gg, mult)
+        tt(blk("Lp", 3), blk("Mp", 2), bb, add)
+        cp(blk("Pp", 0), G(0))
+        cp(blk("Lp", 0), X(0))
+    tt(blk("Lp", 2), blk("Mp", 3), X(2), add)
 
     if r == 0:
-        cp("yh1", blk("ys", 2), blk("Lp", 2))
-        cp("yh0", blk("ys", 0), X(0))
-        cp("yh0", blk("ys", 1), blk("Lp", 1))
+        cp(blk("ys", 0), X(0), "yh0")
+        cp(blk("ys", 1), blk("Lp", 1), "yh0")
+        cp(blk("ys", 2), blk("Lp", 2), "yh1")
         half = {0: ["yh0"], 1: ["yh1", "y3r"]}
     else:
-        if pair_dests:
-            tt("va", blk("Pp", 3), blk("Pp", 2), G(3), mult)
-            tt("vb", blk("Lp", 3), blk("Mp", 2), X(3), add)
-        cp("va", blk("Pp", 0), G(0))
-        cp("vb", blk("Lp", 0), X(0))
-
         def landed(k):
             V.wait_ge(sem["ap%d" % k], engines(k, PAIR_DESTS[k])[1])
             return blk("pland", 2 * (k - 1)), blk("pland", 2 * (k - 1) + 1)
@@ -141,27 +141,27 @@ def rank_program(g, core, T, topo):
             i = 0
             for k in range(r - 2, 0, -1):
                 Ak, bk = landed(k)
-                t = blk("Mp", 3) if d_sbuf else blk("tq", i)
-                tt("vb", t, Q, bk, mult)
-                tt("va", blk("Qp", i), Q, Ak, mult)
-                tt("vb", blk("Dp", i), t, d, add)
+                t = blk("Rp", 0) if d_sbuf else blk("tq", i)
+                tt(blk("Qp", i), Q, Ak, mult)
+                tt(t, Q, bk, mult)
+                if k == 1:
+                    V.wait_ge(sem.av, n_val)
+                    tt(blk("tq", i + 1), blk("Qp", i), val, mult)
+                tt(blk("Dp", i), t, d, add)
                 Q, d, d_sbuf = blk("Qp", i), blk("Dp", i), False
                 i += 1
-            V.wait_ge(sem.av, n_val)
-            t = blk("Mp", 3) if d_sbuf else blk("tq", i)
-            tt("vb", t, Q, val, mult)
+            if r == 2:
+                V.wait_ge(sem.av, n_val)
+                tt(blk("Rp", 0), Q, val, mult)
             c = blk("cs", 0)
-            tt("vb", c, t, d, add)
+            tt(c, blk("Rp", 0) if r == 2 else blk("tq", i), d, add)
 
-        tt("va", blk("ts", 0), blk("Pp", 0), c, mult)
-        tt("va", blk("ts", 1), blk("Pp", 1), c, mult)
-        tt("vb", blk("ts", 2), blk("Pp", 2), c, mult)
-        tt("vb", blk("ts", 3), blk("Pp", 3), c, mult)
-        tt("yh0", blk("ys", 0, 2), blk("ts", 0, 2), blk("Lp", 0, 2), add)
-        tt("yh1", blk("ys", 2, 2), blk("ts", 2, 2), blk("Lp", 2, 2), add)
+        for s in range(S):
+            tt(blk("ts", s), blk("Pp", s), c, mult)
+        tt(blk("ys", 0, 2), blk("ts", 0, 2), blk("Lp", 0, 2), add, "yh0")
+        tt(blk("ys", 2, 2), blk("ts", 2, 2), blk("Lp", 2, 2), add, "yh1")
         half = {0: ["yh0"], 1: ["yh1"]}
-    for s in list(counts):
-        wait_whole(s)
+    need([e[0] for e in dirty])
 
     def send(src, dst, dests, rsem):
         mk, n = engines(r, dests)

@@ -3,7 +3,8 @@ from concourse.mybir import AluOpType
 
 B = 128
 S = 4
-NV = 40
+N = 6
+WMAX = N - 1 + S
 
 VAL_DESTS = {0: [1, 2, 3, 4, 5]}
 PAIR_DESTS = {1: [2, 3, 4, 5], 2: [3, 4, 5], 3: [4, 5], 4: [5]}
@@ -11,24 +12,21 @@ PAIR_DESTS = {1: [2, 3, 4, 5], 2: [3, 4, 5], 3: [4, 5], 4: [5]}
 SCRATCH = {
     "xs": ("sbuf", [128, S * B], "bfloat16"),
     "gs": ("sbuf", [128, S * B], "bfloat16"),
-    "gg": ("sbuf", [128, B], "bfloat16"),
-    "bb": ("sbuf", [128, B], "bfloat16"),
+    "gi": ("sbuf", [128, S * B], "bfloat16"),
+    "ei": ("sbuf", [128, S * B], "bfloat16"),
+    "xi": ("sbuf", [128, S * B], "bfloat16"),
+    "Po": ("sbuf", [128, S * B], "bfloat16"),
+    "Lo": ("sbuf", [128, S * B], "bfloat16"),
     "ab": ("sbuf", [128, 2 * B], "bfloat16"),
-    "ys": ("sbuf", [128, S * B], "bfloat16"),
-    "ts": ("sbuf", [128, S * B], "bfloat16"),
-    "tq": ("sbuf", [128, 4 * B], "bfloat16"),
-    "cs": ("sbuf", [128, B], "bfloat16"),
     "pland": ("sbuf", [128, 4 * 2 * B], "bfloat16"),
     "vland": ("sbuf", [128, B], "bfloat16"),
-    "Pp": ("psum", [128, S * B], "float32"),
-    "Lp": ("psum", [128, S * B], "float32"),
-    "Mp": ("psum", [128, 4 * B], "float32"),
-    "Rp": ("psum", [128, B], "float32"),
-    "Qp": ("psum", [128, 4 * B], "float32"),
-    "Dp": ("psum", [128, 4 * B], "float32"),
+    "D0": ("sbuf", [128, WMAX * B], "bfloat16"),
+    "D1": ("sbuf", [128, WMAX * B], "bfloat16"),
+    "Oo": ("sbuf", [128, WMAX * B], "bfloat16"),
+    "ys": ("sbuf", [128, S * B], "bfloat16"),
 }
-SEMAPHORES = ["ldx", "ldg", "abr", "y3r", "yh0", "yh1", "st0", "st1", "sent", "av",
-              "ap1", "ap2", "ap3", "ap4"] + ["s%d" % i for i in range(NV)]
+SEMAPHORES = ["ldx", "ldg", "zz", "cg", "cx", "sp", "sl", "abr", "y3r", "cd", "ca", "so", "yh0", "yh1",
+              "st0", "st1", "sent", "av", "ap1", "ap2", "ap3", "ap4"]
 
 
 def rank_program(g, core, T, topo):
@@ -41,6 +39,8 @@ def rank_program(g, core, T, topo):
     mult, add = AluOpType.mult, AluOpType.add
     val_dests = VAL_DESTS.get(r, [])
     pair_dests = PAIR_DESTS.get(r, [])
+    sender = bool(val_dests or pair_dests)
+    W = r + S
 
     def engines(src_rank, dests):
         mk = None
@@ -56,112 +56,78 @@ def rank_program(g, core, T, topo):
     g.scalar.dma_start(T.xs[:], T.x[:]).then_inc(sem.ldx, 16)
 
     counts = {}
-    dirty = []
 
-    def ap(rg):
-        return T[rg[0]][:, rg[1]:rg[2]]
-
-    def blk(name, i, n=1):
-        return (name, i * B, (i + n) * B)
-
-    def need(regs):
-        for a in regs:
-            for e in list(dirty):
-                d = e[0]
-                if a[0] == d[0] and a[1] < d[2] and d[1] < a[2] and e in dirty:
-                    V.wait_ge(sem[e[1]], counts[e[1]])
-                    dirty[:] = [f for f in dirty if f[1] != e[1]]
-
-    def done(ins, out, s):
-        if s is None:
-            s = "s%d" % len([q for q in counts if q[0] == "s" and q[1:].isdigit()])
+    def inc(ins, s):
         ins.then_inc(sem[s], 1)
         counts[s] = counts.get(s, 0) + 1
-        dirty.append((out, s))
 
-    def tt(out, a, b, op, s=None):
-        need([a, b, out])
-        done(V.tensor_tensor(ap(out), ap(a), ap(b), op), out, s)
+    def vwait(*names):
+        for s in names:
+            if counts.get(s, 0):
+                V.wait_ge(sem[s], counts[s])
 
-    def cp(out, a, s=None):
-        need([a, out])
-        done(V.tensor_copy(ap(out), ap(a)), out, s)
+    def plain(name, i):
+        return T[name][:, i * B:(i + 1) * B]
 
-    def G(i):
-        return blk("gs", i)
+    def slot(name, k, w):
+        return T[name][:, k:w * B:w]
 
-    def X(i):
-        return blk("xs", i)
-
-    gg, bb = blk("gg", 0), blk("bb", 0)
+    if sender:
+        inc(V.memset(slot("gi", 0, S), 0.0), "zz")
+        if r > 0:
+            inc(V.memset(T.ei[:], 0.0), "zz")
+    if r > 0:
+        inc(V.memset(slot("D0", 0, W), 0.0), "cd")
 
     V.wait_ge(sem.ldg, 16)
-    V.wait_ge(sem.ldx, 16)
-    tt(blk("Mp", 0), G(1), X(0), mult)
-    tt(gg, G(2), G(3), mult)
-    tt(blk("Mp", 1), G(3), X(2), mult)
-    tt(blk("Lp", 1), blk("Mp", 0), X(1), add)
-    if r > 0:
-        tt(blk("Pp", 1), G(0), G(1), mult)
-    tt(bb, blk("Mp", 1), X(3), add)
-    tt(blk("Mp", 2), blk("Lp", 1), gg, mult)
-    if pair_dests:
-        tt(blk("ab", 0), blk("Pp", 1), gg, mult, "abr")
-        tt(blk("ab", 1), blk("Mp", 2), bb, add, "abr")
-    if r == 0:
-        tt(blk("ys", 3), blk("Mp", 2), bb, add, "y3r")
-
-    tt(blk("Mp", 3), blk("Lp", 1), G(2), mult)
-    if r > 0:
-        tt(blk("Pp", 2), blk("Pp", 1), G(2), mult)
-        tt(blk("Pp", 3), blk("Pp", 1), gg, mult)
-        tt(blk("Lp", 3), blk("Mp", 2), bb, add)
-        cp(blk("Pp", 0), G(0))
-        cp(blk("Lp", 0), X(0))
-    tt(blk("Lp", 2), blk("Mp", 3), X(2), add)
+    if sender:
+        vwait("zz")
+        if r > 0:
+            inc(V.tensor_copy(slot("ei", 0, S), plain("gs", 0)), "cg")
+        for s in range(1, S):
+            inc(V.tensor_copy(slot("gi", s, S), plain("gs", s)), "cg")
+        V.wait_ge(sem.ldx, 16)
+        for s in range(S):
+            inc(V.tensor_copy(slot("xi", s, S), plain("xs", s)), "cx")
+        vwait("cg")
+        if r > 0:
+            inc(V.tensor_tensor_scan(T.Po[:], T.gi[:], T.ei[:], 0.0, mult, add), "sp")
+        vwait("cx")
+        inc(V.tensor_tensor_scan(T.Lo[:], T.gi[:], T.xi[:], 0.0, mult, add), "sl")
+        if r > 0:
+            vwait("sp")
+            inc(V.tensor_copy(plain("ab", 0), slot("Po", S - 1, S)), "abr")
+            vwait("sl")
+            inc(V.tensor_copy(plain("ab", 1), slot("Lo", S - 1, S)), "abr")
+    else:
+        V.wait_ge(sem.ldx, 16)
 
     if r == 0:
-        cp(blk("ys", 0), X(0), "yh0")
-        cp(blk("ys", 1), blk("Lp", 1), "yh0")
-        cp(blk("ys", 2), blk("Lp", 2), "yh1")
+        vwait("sl")
+        inc(V.tensor_copy(plain("ys", 3), slot("Lo", 3, S)), "y3r")
+        inc(V.tensor_copy(plain("ys", 2), slot("Lo", 2, S)), "yh1")
+        inc(V.tensor_copy(plain("ys", 0), slot("Lo", 0, S)), "yh0")
+        inc(V.tensor_copy(plain("ys", 1), slot("Lo", 1, S)), "yh0")
         half = {0: ["yh0"], 1: ["yh1", "y3r"]}
     else:
-        def landed(k):
-            V.wait_ge(sem["ap%d" % k], engines(k, PAIR_DESTS[k])[1])
-            return blk("pland", 2 * (k - 1)), blk("pland", 2 * (k - 1) + 1)
-
-        n_val = engines(0, VAL_DESTS[0])[1]
-        val = blk("vland", 0)
-        if r == 1:
-            V.wait_ge(sem.av, n_val)
-            c = val
-        else:
-            Q, d = landed(r - 1)
-            d_sbuf = True
-            i = 0
-            for k in range(r - 2, 0, -1):
-                Ak, bk = landed(k)
-                t = blk("Rp", 0) if d_sbuf else blk("tq", i)
-                tt(blk("Qp", i), Q, Ak, mult)
-                tt(t, Q, bk, mult)
-                if k == 1:
-                    V.wait_ge(sem.av, n_val)
-                    tt(blk("tq", i + 1), blk("Qp", i), val, mult)
-                tt(blk("Dp", i), t, d, add)
-                Q, d, d_sbuf = blk("Qp", i), blk("Dp", i), False
-                i += 1
-            if r == 2:
-                V.wait_ge(sem.av, n_val)
-                tt(blk("Rp", 0), Q, val, mult)
-            c = blk("cs", 0)
-            tt(c, blk("Rp", 0) if r == 2 else blk("tq", i), d, add)
-
         for s in range(S):
-            tt(blk("ts", s), blk("Pp", s), c, mult)
-        tt(blk("ys", 0, 2), blk("ts", 0, 2), blk("Lp", 0, 2), add, "yh0")
-        tt(blk("ys", 2, 2), blk("ts", 2, 2), blk("Lp", 2, 2), add, "yh1")
+            inc(V.tensor_copy(slot("D0", r + s, W), plain("gs", s)), "cd")
+            inc(V.tensor_copy(slot("D1", r + s, W), plain("xs", s)), "cd")
+        order = list(range(r - 1, 1, -1)) + [0] + ([1] if r > 1 else [])
+        for k in order:
+            if k == 0:
+                V.wait_ge(sem.av, engines(0, VAL_DESTS[0])[1])
+                inc(V.tensor_copy(slot("D1", 0, W), T.vland[:]), "ca")
+            else:
+                V.wait_ge(sem["ap%d" % k], engines(k, PAIR_DESTS[k])[1])
+                inc(V.tensor_copy(slot("D0", k, W), plain("pland", 2 * (k - 1))), "ca")
+                inc(V.tensor_copy(slot("D1", k, W), plain("pland", 2 * (k - 1) + 1)), "ca")
+        vwait("cd", "ca")
+        inc(V.tensor_tensor_scan(T.Oo[:, 0:W * B], T.D0[:, 0:W * B], T.D1[:, 0:W * B], 0.0, mult, add), "so")
+        vwait("so")
+        for s in range(S):
+            inc(V.tensor_copy(plain("ys", s), slot("Oo", r + s, W)), "yh%d" % (s // 2))
         half = {0: ["yh0"], 1: ["yh1"]}
-    need([e[0] for e in dirty])
 
     def send(src, dst, dests, rsem):
         mk, n = engines(r, dests)
@@ -169,16 +135,16 @@ def rank_program(g, core, T, topo):
         for j in dests:
             a = topo.addr(cores[j])
             ids.append(DstId(rid=a[0], pnc=a[1]))
-        g.remote_dma_fused([RemoteDMATransfer(dst_ids=ids, dma_engine_mask=mk, remote_sem=rsem, srcs=[ap(src)],
-                                              dsts=[ap(dst) for j in dests], alu_op=0)], local_sem=sem.sent)
+        g.remote_dma_fused([RemoteDMATransfer(dst_ids=ids, dma_engine_mask=mk, remote_sem=rsem, srcs=[src],
+                                              dsts=[dst for j in dests], alu_op=0)], local_sem=sem.sent)
         return n
 
     if pair_dests:
         g.wait_ge(sem.abr, counts["abr"])
-        g.wait_ge(sem.sent, send(blk("ab", 0, 2), blk("pland", 2 * (r - 1), 2), pair_dests, sem["ap%d" % r]))
+        g.wait_ge(sem.sent, send(T.ab[:], T.pland[:, 2 * (r - 1) * B:2 * r * B], pair_dests, sem["ap%d" % r]))
     if val_dests:
         g.wait_ge(sem.y3r, counts["y3r"])
-        g.wait_ge(sem.sent, send(blk("ys", 3), blk("vland", 0), val_dests, sem.av))
+        g.wait_ge(sem.sent, send(plain("ys", 3), T.vland[:], val_dests, sem.av))
 
     for h, q, st in ((0, g.sync, sem.st0), (1, g.scalar, sem.st1)):
         for s in half[h]:

@@ -1,13 +1,18 @@
 from concourse.bass import DstId, RemoteDMATransfer
-from concourse.mybir import AluOpType
+from concourse.mybir import AluOpType, ActivationFunctionType
 
 B = 128
 S = 4
 N = 6
-WMAX = N - 1 + S
+WMAX = N + S
 
-VAL_DESTS = {0: [1, 2, 3, 4, 5]}
-PAIR_DESTS = {1: [2, 3, 4, 5], 2: [3, 4, 5], 3: [4, 5], 4: [5]}
+MAIN = {1: [("far", [5, 3], 2), ("far", [4], 1), ("next", [2], 1)],
+        2: [("far", [5, 4], 1), ("next", [3], 1)],
+        3: [("far", [5], 1), ("next", [4], 1)],
+        4: [("next", [5], 1)]}
+FAR0 = [2, 3, 4, 5]
+SCALAR_GATES = (2, 3, 4)
+ORDER = {1: [0], 2: [0, 1], 3: [0, 2, 1], 4: [3, 0, 2, 1], 5: [4, 3, 2, 1, 0]}
 
 SCRATCH = {
     "xs": ("sbuf", [128, S * B], "bfloat16"),
@@ -17,16 +22,18 @@ SCRATCH = {
     "xi": ("sbuf", [128, S * B], "bfloat16"),
     "Po": ("sbuf", [128, S * B], "bfloat16"),
     "Lo": ("sbuf", [128, S * B], "bfloat16"),
-    "ab": ("sbuf", [128, 2 * B], "bfloat16"),
-    "pland": ("sbuf", [128, 4 * 2 * B], "bfloat16"),
+    "ab": ("sbuf", [128, 3 * B], "bfloat16"),
+    "pland": ("sbuf", [128, 3 * 2 * B], "bfloat16"),
+    "sland": ("sbuf", [128, 2 * B], "bfloat16"),
+    "eland": ("sbuf", [128, 2 * B], "bfloat16"),
     "vland": ("sbuf", [128, B], "bfloat16"),
     "D0": ("sbuf", [128, WMAX * B], "bfloat16"),
     "D1": ("sbuf", [128, WMAX * B], "bfloat16"),
     "Oo": ("sbuf", [128, WMAX * B], "bfloat16"),
     "ys": ("sbuf", [128, S * B], "bfloat16"),
 }
-SEMAPHORES = ["ldx", "ldg", "zz", "cg", "cx", "sp", "sl", "abr", "y3r", "cd", "ca", "so", "yh0", "yh1",
-              "st0", "st1", "sent", "av", "ap1", "ap2", "ap3", "ap4"]
+SEMAPHORES = ["ldx", "ldg", "zz", "cg", "cx", "sp", "sl", "abr", "y3r", "y2r", "cd", "ca", "so", "yh0", "yh1",
+              "st0", "st1", "sent", "kg", "kx", "ka", "ky", "ae", "asp", "av", "ap1", "ap2", "ap3"]
 
 
 def rank_program(g, core, T, topo):
@@ -34,26 +41,45 @@ def rank_program(g, core, T, topo):
     if r is None:
         return
     V = g.vector
+    C = g.scalar
     sem = T.sem
     cores = T.cores
     mult, add = AluOpType.mult, AluOpType.add
-    val_dests = VAL_DESTS.get(r, [])
-    pair_dests = PAIR_DESTS.get(r, [])
-    sender = bool(val_dests or pair_dests)
-    W = r + S
+    sender = r < N - 1
+    W = r + 1 + S
 
-    def engines(src_rank, dests):
+    def engines(k):
         mk = None
-        for j in dests:
-            if not topo.may_write(cores[src_rank], cores[j]):
-                raise ValueError("rank %d may not write to rank %d" % (src_rank, j))
-            one = topo.mask(cores[src_rank], cores[j])
+        for j in range(k + 1, N):
+            if not topo.may_write(cores[k], cores[j]):
+                raise ValueError("rank %d may not write to rank %d" % (k, j))
+            one = topo.mask(cores[k], cores[j])
             mk = one if mk is None else (mk & one)
-        return mk, bin(mk).count("1")
+        return [i for i in range(mk.bit_length()) if (mk >> i) & 1]
+
+    def groups(k, shares):
+        eng = engines(k)
+        unit = len(eng) // sum(shares)
+        out, pos = [], 0
+        for sh in shares:
+            part = eng[pos:pos + sh * unit]
+            pos += sh * unit
+            out.append((sum(1 << i for i in part), len(part)))
+        return out
+
+    def main_plan(k):
+        gr = groups(k, [t[2] for t in MAIN[k]])
+        return [(t[0], t[1], m[0], m[1]) for t, m in zip(MAIN[k], gr)]
+
+    def due(k, j):
+        for kind, dests, mk, n in main_plan(k):
+            if j in dests:
+                return n
+        raise ValueError("no write from %d to %d" % (k, j))
 
     g0 = 0 if r > 0 else B
     g.sync.dma_start(T.gs[:, g0:S * B], T.gate[:, g0:S * B]).then_inc(sem.ldg, 16)
-    g.scalar.dma_start(T.xs[:], T.x[:]).then_inc(sem.ldx, 16)
+    C.dma_start(T.xs[:], T.x[:]).then_inc(sem.ldx, 16)
 
     counts = {}
 
@@ -65,6 +91,14 @@ def rank_program(g, core, T, topo):
         for s in names:
             if counts.get(s, 0):
                 V.wait_ge(sem[s], counts[s])
+
+    def cwait(*names):
+        for s in names:
+            if counts.get(s, 0):
+                C.wait_ge(sem[s], counts[s])
+
+    def ccopy(out, in_, s):
+        inc(C.activation(out, in_, ActivationFunctionType.Copy), s)
 
     def plain(name, i):
         return T[name][:, i * B:(i + 1) * B]
@@ -78,25 +112,34 @@ def rank_program(g, core, T, topo):
             inc(V.memset(T.ei[:], 0.0), "zz")
     if r > 0:
         inc(V.memset(slot("D0", 0, W), 0.0), "cd")
+    if r > 1:
+        inc(V.memset(slot("D1", r - 1, W), 0.0), "cd")
 
     V.wait_ge(sem.ldg, 16)
     if sender:
         vwait("zz")
         if r > 0:
-            inc(V.tensor_copy(slot("ei", 0, S), plain("gs", 0)), "cg")
+            C.wait_ge(sem.ldg, 16)
+            cwait("zz")
+            ccopy(slot("ei", 0, S), plain("gs", 0), "kg")
+        C.wait_ge(sem.ldx, 16)
+        for s in range(S - 2, S):
+            ccopy(slot("xi", s, S), plain("xs", s), "kx")
         for s in range(1, S):
             inc(V.tensor_copy(slot("gi", s, S), plain("gs", s)), "cg")
         V.wait_ge(sem.ldx, 16)
-        for s in range(S):
+        for s in range(S - 2):
             inc(V.tensor_copy(slot("xi", s, S), plain("xs", s)), "cx")
-        vwait("cg")
+        vwait("cg", "kg")
         if r > 0:
             inc(V.tensor_tensor_scan(T.Po[:], T.gi[:], T.ei[:], 0.0, mult, add), "sp")
-        vwait("cx")
+        vwait("cx", "kx")
         inc(V.tensor_tensor_scan(T.Lo[:], T.gi[:], T.xi[:], 0.0, mult, add), "sl")
         if r > 0:
             vwait("sp")
-            inc(V.tensor_copy(plain("ab", 0), slot("Po", S - 1, S)), "abr")
+            inc(V.tensor_copy(plain("ab", 0), slot("Po", S - 2, S)), "abr")
+            if any(t[0] == "far" for t in MAIN[r]):
+                inc(V.tensor_copy(plain("ab", 2), slot("Po", S - 1, S)), "abr")
             vwait("sl")
             inc(V.tensor_copy(plain("ab", 1), slot("Lo", S - 1, S)), "abr")
     else:
@@ -105,48 +148,88 @@ def rank_program(g, core, T, topo):
     if r == 0:
         vwait("sl")
         inc(V.tensor_copy(plain("ys", 3), slot("Lo", 3, S)), "y3r")
-        inc(V.tensor_copy(plain("ys", 2), slot("Lo", 2, S)), "yh1")
+        inc(V.tensor_copy(plain("ys", 2), slot("Lo", 2, S)), "y2r")
         inc(V.tensor_copy(plain("ys", 0), slot("Lo", 0, S)), "yh0")
         inc(V.tensor_copy(plain("ys", 1), slot("Lo", 1, S)), "yh0")
-        half = {0: ["yh0"], 1: ["yh1", "y3r"]}
+        half = {0: ["yh0"], 1: ["y2r", "y3r"]}
     else:
         for s in range(S):
-            inc(V.tensor_copy(slot("D0", r + s, W), plain("gs", s)), "cd")
-            inc(V.tensor_copy(slot("D1", r + s, W), plain("xs", s)), "cd")
-        order = list(range(r - 1, 1, -1)) + [0] + ([1] if r > 1 else [])
-        for k in order:
+            inc(V.tensor_copy(slot("D0", r + 1 + s, W), plain("gs", s)), "cd")
+            inc(V.tensor_copy(slot("D1", r + 1 + s, W), plain("xs", s)), "cd")
+        V.wait_ge(sem.ae, len(engines(r - 1)))
+        inc(V.tensor_copy(slot("D0", r, W), plain("eland", 0)), "ca")
+        if r == 1:
+            inc(V.tensor_copy(slot("D1", r, W), plain("eland", 1)), "ca")
+        for k in ORDER[r]:
             if k == 0:
-                V.wait_ge(sem.av, engines(0, VAL_DESTS[0])[1])
+                V.wait_ge(sem.asp if r == 1 else sem.av, len(engines(0)))
                 inc(V.tensor_copy(slot("D1", 0, W), T.vland[:]), "ca")
+            elif k == r - 1:
+                V.wait_ge(sem.asp, due(k, r))
+                inc(V.tensor_copy(slot("D1", r, W), plain("sland", 1)), "ca")
+                if k in SCALAR_GATES:
+                    C.wait_ge(sem.asp, due(k, r))
+                    ccopy(slot("D0", r - 1, W), plain("sland", 0), "ka")
+                else:
+                    inc(V.tensor_copy(slot("D0", r - 1, W), plain("sland", 0)), "ca")
             else:
-                V.wait_ge(sem["ap%d" % k], engines(k, PAIR_DESTS[k])[1])
-                inc(V.tensor_copy(slot("D0", k, W), plain("pland", 2 * (k - 1))), "ca")
-                inc(V.tensor_copy(slot("D1", k, W), plain("pland", 2 * (k - 1) + 1)), "ca")
-        vwait("cd", "ca")
+                V.wait_ge(sem["ap%d" % k], due(k, r))
+                inc(V.tensor_copy(slot("D1", k, W), plain("pland", 2 * (k - 1))), "ca")
+                if k in SCALAR_GATES:
+                    C.wait_ge(sem["ap%d" % k], due(k, r))
+                    ccopy(slot("D0", k, W), plain("pland", 2 * (k - 1) + 1), "ka")
+                else:
+                    inc(V.tensor_copy(slot("D0", k, W), plain("pland", 2 * (k - 1) + 1)), "ca")
+        vwait("cd", "ca", "ka")
         inc(V.tensor_tensor_scan(T.Oo[:, 0:W * B], T.D0[:, 0:W * B], T.D1[:, 0:W * B], 0.0, mult, add), "so")
         vwait("so")
-        for s in range(S):
-            inc(V.tensor_copy(plain("ys", s), slot("Oo", r + s, W)), "yh%d" % (s // 2))
-        half = {0: ["yh0"], 1: ["yh1"]}
+        cwait("so")
+        ccopy(plain("ys", S - 1), slot("Oo", r + S, W), "ky")
+        for s in range(S - 1):
+            inc(V.tensor_copy(plain("ys", s), slot("Oo", r + 1 + s, W)), "yh%d" % (s // 2))
+        half = {0: ["yh0"], 1: ["yh1", "ky"]}
 
-    def send(src, dst, dests, rsem):
-        mk, n = engines(r, dests)
+    def transfer(src, dst, dests, mk, rsem):
         ids = []
         for j in dests:
             a = topo.addr(cores[j])
             ids.append(DstId(rid=a[0], pnc=a[1]))
-        g.remote_dma_fused([RemoteDMATransfer(dst_ids=ids, dma_engine_mask=mk, remote_sem=rsem, srcs=[src],
-                                              dsts=[dst for j in dests], alu_op=0)], local_sem=sem.sent)
-        return n
+        return RemoteDMATransfer(dst_ids=ids, dma_engine_mask=mk, remote_sem=rsem, srcs=[src],
+                                 dsts=[dst for j in dests], alu_op=0)
 
-    if pair_dests:
-        g.wait_ge(sem.abr, counts["abr"])
-        g.wait_ge(sem.sent, send(T.ab[:], T.pland[:, 2 * (r - 1) * B:2 * r * B], pair_dests, sem["ap%d" % r]))
-    if val_dests:
-        g.wait_ge(sem.y3r, counts["y3r"])
-        g.wait_ge(sem.sent, send(plain("ys", 3), T.vland[:], val_dests, sem.av))
+    left = 0
+    if sender:
+        g.wait_ge(sem.ldg, 16)
+        if r == 0:
+            g.wait_ge(sem.ldx, 16)
+            (m0, n0), (m1, n1) = groups(0, [1, 1])
+            g.remote_dma_fused([transfer(plain("gs", 3), plain("eland", 0), [1], m0, sem.ae),
+                                transfer(plain("xs", 3), plain("eland", 1), [1], m1, sem.ae)], local_sem=sem.sent)
+            left += n0 + n1
+            (mk, n), = groups(0, [1])
+            g.wait_ge(sem.y3r, counts["y3r"])
+            g.remote_dma_fused([transfer(plain("ys", 3), T.vland[:], FAR0, mk, sem.av)], local_sem=sem.sent)
+            g.wait_ge(sem.y2r, counts["y2r"])
+            g.remote_dma_fused([transfer(plain("ys", 2), T.vland[:], [1], mk, sem.asp)], local_sem=sem.sent)
+            left += 2 * n
+        else:
+            (mk, n), = groups(r, [1])
+            g.remote_dma_fused([transfer(plain("gs", 3), plain("eland", 0), [r + 1], mk, sem.ae)],
+                               local_sem=sem.sent)
+            left += n
+            trs = []
+            for kind, dests, mk, n in main_plan(r):
+                if kind == "far":
+                    trs.append(transfer(T.ab[:, B:3 * B], T.pland[:, 2 * (r - 1) * B:2 * r * B], dests, mk,
+                                        sem["ap%d" % r]))
+                else:
+                    trs.append(transfer(T.ab[:, 0:2 * B], T.sland[:], dests, mk, sem.asp))
+                left += n
+            g.wait_ge(sem.abr, counts["abr"])
+            g.remote_dma_fused(trs, local_sem=sem.sent)
+        g.wait_ge(sem.sent, left)
 
-    for h, q, st in ((0, g.sync, sem.st0), (1, g.scalar, sem.st1)):
+    for h, q, st in ((0, g.sync, sem.st0), (1, C, sem.st1)):
         for s in half[h]:
             q.wait_ge(sem[s], counts[s])
         q.dma_start(T.y[:, 2 * h * B:(2 * h + 2) * B], T.ys[:, 2 * h * B:(2 * h + 2) * B]).then_inc(st, 16)

from concourse.bass import DstId, RemoteDMATransfer
from concourse.mybir import AluOpType, ActivationFunctionType

B = 128
S = 4
N = 6
WMAX = N + S

MAIN = {1: [("far", [5, 3], 2), ("far", [4], 1), ("next", [2], 1)],
        2: [("far", [5, 4], 1), ("next", [3], 1)],
        3: [("far", [5], 1), ("next", [4], 1)],
        4: [("next", [5], 1)]}
FAR0 = [2, 3, 4, 5]
SCALAR_GATES = (2, 3, 4)
ORDER = {1: [0], 2: [0, 1], 3: [0, 2, 1], 4: [3, 0, 2, 1], 5: [4, 3, 2, 1, 0]}

SCRATCH = {
    "xs": ("sbuf", [128, S * B], "bfloat16"),
    "gs": ("sbuf", [128, S * B], "bfloat16"),
    "gi": ("sbuf", [128, S * B], "bfloat16"),
    "ei": ("sbuf", [128, S * B], "bfloat16"),
    "xi": ("sbuf", [128, S * B], "bfloat16"),
    "Po": ("sbuf", [128, S * B], "bfloat16"),
    "Lo": ("sbuf", [128, S * B], "bfloat16"),
    "ab": ("sbuf", [128, 3 * B], "bfloat16"),
    "pland": ("sbuf", [128, 3 * 2 * B], "bfloat16"),
    "sland": ("sbuf", [128, 2 * B], "bfloat16"),
    "eland": ("sbuf", [128, 2 * B], "bfloat16"),
    "vland": ("sbuf", [128, B], "bfloat16"),
    "D0": ("sbuf", [128, WMAX * B], "bfloat16"),
    "D1": ("sbuf", [128, WMAX * B], "bfloat16"),
    "Oo": ("sbuf", [128, WMAX * B], "bfloat16"),
    "ys": ("sbuf", [128, S * B], "bfloat16"),
}
SEMAPHORES = ["ldx", "ldg", "zz", "cg", "cx", "sp", "sl", "abr", "y3r", "y2r", "cd", "ca", "so", "yh0", "yh1",
              "st0", "st1", "sent", "kg", "kx", "ka", "ky", "ae", "asp", "av", "ap1", "ap2", "ap3"]


def rank_program(g, core, T, topo):
    r = T.rank_of(core)
    if r is None:
        return
    V = g.vector
    C = g.scalar
    sem = T.sem
    cores = T.cores
    mult, add = AluOpType.mult, AluOpType.add
    sender = r < N - 1
    W = r + 1 + S

    def engines(k):
        mk = None
        for j in range(k + 1, N):
            if not topo.may_write(cores[k], cores[j]):
                raise ValueError("rank %d may not write to rank %d" % (k, j))
            one = topo.mask(cores[k], cores[j])
            mk = one if mk is None else (mk & one)
        return [i for i in range(mk.bit_length()) if (mk >> i) & 1]

    def groups(k, shares):
        eng = engines(k)
        unit = len(eng) // sum(shares)
        out, pos = [], 0
        for sh in shares:
            part = eng[pos:pos + sh * unit]
            pos += sh * unit
            out.append((sum(1 << i for i in part), len(part)))
        return out

    def main_plan(k):
        gr = groups(k, [t[2] for t in MAIN[k]])
        return [(t[0], t[1], m[0], m[1]) for t, m in zip(MAIN[k], gr)]

    def due(k, j):
        for kind, dests, mk, n in main_plan(k):
            if j in dests:
                return n
        raise ValueError("no write from %d to %d" % (k, j))

    g0 = 0 if r > 0 else B
    g.sync.dma_start(T.gs[:, g0:S * B], T.gate[:, g0:S * B]).then_inc(sem.ldg, 16)
    C.dma_start(T.xs[:], T.x[:]).then_inc(sem.ldx, 16)

    counts = {}

    def inc(ins, s):
        ins.then_inc(sem[s], 1)
        counts[s] = counts.get(s, 0) + 1

    def vwait(*names):
        for s in names:
            if counts.get(s, 0):
                V.wait_ge(sem[s], counts[s])

    def cwait(*names):
        for s in names:
            if counts.get(s, 0):
                C.wait_ge(sem[s], counts[s])

    def ccopy(out, in_, s):
        inc(C.activation(out, in_, ActivationFunctionType.Copy), s)

    def plain(name, i):
        return T[name][:, i * B:(i + 1) * B]

    def slot(name, k, w):
        return T[name][:, k:w * B:w]

    if sender:
        inc(V.memset(slot("gi", 0, S), 0.0), "zz")
        if r > 0:
            inc(V.memset(T.ei[:], 0.0), "zz")
    if r > 0:
        inc(V.memset(slot("D0", 0, W), 0.0), "cd")
    if r > 1:
        inc(V.memset(slot("D1", r - 1, W), 0.0), "cd")

    V.wait_ge(sem.ldg, 16)
    if sender:
        vwait("zz")
        if r > 0:
            C.wait_ge(sem.ldg, 16)
            cwait("zz")
            ccopy(slot("ei", 0, S), plain("gs", 0), "kg")
        C.wait_ge(sem.ldx, 16)
        for s in range(S - 2, S):
            ccopy(slot("xi", s, S), plain("xs", s), "kx")
        for s in range(1, S):
            inc(V.tensor_copy(slot("gi", s, S), plain("gs", s)), "cg")
        V.wait_ge(sem.ldx, 16)
        for s in range(S - 2):
            inc(V.tensor_copy(slot("xi", s, S), plain("xs", s)), "cx")
        vwait("cg", "kg")
        if r > 0:
            inc(V.tensor_tensor_scan(T.Po[:], T.gi[:], T.ei[:], 0.0, mult, add), "sp")
        vwait("cx", "kx")
        inc(V.tensor_tensor_scan(T.Lo[:], T.gi[:], T.xi[:], 0.0, mult, add), "sl")
        if r > 0:
            vwait("sp")
            inc(V.tensor_copy(plain("ab", 0), slot("Po", S - 2, S)), "abr")
            if any(t[0] == "far" for t in MAIN[r]):
                inc(V.tensor_copy(plain("ab", 2), slot("Po", S - 1, S)), "abr")
            vwait("sl")
            inc(V.tensor_copy(plain("ab", 1), slot("Lo", S - 1, S)), "abr")
    else:
        V.wait_ge(sem.ldx, 16)

    if r == 0:
        vwait("sl")
        inc(V.tensor_copy(plain("ys", 3), slot("Lo", 3, S)), "y3r")
        inc(V.tensor_copy(plain("ys", 2), slot("Lo", 2, S)), "y2r")
        inc(V.tensor_copy(plain("ys", 0), slot("Lo", 0, S)), "yh0")
        inc(V.tensor_copy(plain("ys", 1), slot("Lo", 1, S)), "yh0")
        half = {0: ["yh0"], 1: ["y2r", "y3r"]}
    else:
        for s in range(S):
            inc(V.tensor_copy(slot("D0", r + 1 + s, W), plain("gs", s)), "cd")
            inc(V.tensor_copy(slot("D1", r + 1 + s, W), plain("xs", s)), "cd")
        V.wait_ge(sem.ae, len(engines(r - 1)))
        inc(V.tensor_copy(slot("D0", r, W), plain("eland", 0)), "ca")
        if r == 1:
            inc(V.tensor_copy(slot("D1", r, W), plain("eland", 1)), "ca")
        for k in ORDER[r]:
            if k == 0:
                V.wait_ge(sem.asp if r == 1 else sem.av, len(engines(0)))
                inc(V.tensor_copy(slot("D1", 0, W), T.vland[:]), "ca")
            elif k == r - 1:
                V.wait_ge(sem.asp, due(k, r))
                inc(V.tensor_copy(slot("D1", r, W), plain("sland", 1)), "ca")
                if k in SCALAR_GATES:
                    C.wait_ge(sem.asp, due(k, r))
                    ccopy(slot("D0", r - 1, W), plain("sland", 0), "ka")
                else:
                    inc(V.tensor_copy(slot("D0", r - 1, W), plain("sland", 0)), "ca")
            else:
                V.wait_ge(sem["ap%d" % k], due(k, r))
                inc(V.tensor_copy(slot("D1", k, W), plain("pland", 2 * (k - 1))), "ca")
                if k in SCALAR_GATES:
                    C.wait_ge(sem["ap%d" % k], due(k, r))
                    ccopy(slot("D0", k, W), plain("pland", 2 * (k - 1) + 1), "ka")
                else:
                    inc(V.tensor_copy(slot("D0", k, W), plain("pland", 2 * (k - 1) + 1)), "ca")
        vwait("cd", "ca", "ka")
        inc(V.tensor_tensor_scan(T.Oo[:, 0:W * B], T.D0[:, 0:W * B], T.D1[:, 0:W * B], 0.0, mult, add), "so")
        vwait("so")
        cwait("so")
        ccopy(plain("ys", S - 1), slot("Oo", r + S, W), "ky")
        for s in range(S - 1):
            inc(V.tensor_copy(plain("ys", s), slot("Oo", r + 1 + s, W)), "yh%d" % (s // 2))
        half = {0: ["yh0"], 1: ["yh1", "ky"]}

    def transfer(src, dst, dests, mk, rsem):
        ids = []
        for j in dests:
            a = topo.addr(cores[j])
            ids.append(DstId(rid=a[0], pnc=a[1]))
        return RemoteDMATransfer(dst_ids=ids, dma_engine_mask=mk, remote_sem=rsem, srcs=[src],
                                 dsts=[dst for j in dests], alu_op=0)

    left = 0
    if sender:
        g.wait_ge(sem.ldg, 16)
        if r == 0:
            g.wait_ge(sem.ldx, 16)
            (m0, n0), (m1, n1) = groups(0, [1, 1])
            g.remote_dma_fused([transfer(plain("gs", 3), plain("eland", 0), [1], m0, sem.ae),
                                transfer(plain("xs", 3), plain("eland", 1), [1], m1, sem.ae)], local_sem=sem.sent)
            left += n0 + n1
            (mk, n), = groups(0, [1])
            g.wait_ge(sem.y3r, counts["y3r"])
            g.remote_dma_fused([transfer(plain("ys", 3), T.vland[:], FAR0, mk, sem.av)], local_sem=sem.sent)
            g.wait_ge(sem.y2r, counts["y2r"])
            g.remote_dma_fused([transfer(plain("ys", 2), T.vland[:], [1], mk, sem.asp)], local_sem=sem.sent)
            left += 2 * n
        else:
            (mk, n), = groups(r, [1])
            g.remote_dma_fused([transfer(plain("gs", 3), plain("eland", 0), [r + 1], mk, sem.ae)],
                               local_sem=sem.sent)
            left += n
            trs = []
            for kind, dests, mk, n in main_plan(r):
                if kind == "far":
                    trs.append(transfer(T.ab[:, B:3 * B], T.pland[:, 2 * (r - 1) * B:2 * r * B], dests, mk,
                                        sem["ap%d" % r]))
                else:
                    trs.append(transfer(T.ab[:, 0:2 * B], T.sland[:], dests, mk, sem.asp))
                left += n
            g.wait_ge(sem.abr, counts["abr"])
            g.remote_dma_fused(trs, local_sem=sem.sent)
        g.wait_ge(sem.sent, left)

    for h, q, st in ((0, g.sync, sem.st0), (1, C, sem.st1)):
        for s in half[h]:
            q.wait_ge(sem[s], counts[s])
        q.dma_start(T.y[:, 2 * h * B:(2 * h + 2) * B], T.ys[:, 2 * h * B:(2 * h + 2) * B]).then_inc(st, 16)
        q.wait_ge(st, 16)
